import numpy as np, ml_dtypes
CORES = [35,38,43,46]
N = 4
WB, F = 1, 64
def setup_inputs(rng):
    return {"a": rng.standard_normal((N, 128, 128), dtype=np.float32).astype(ml_dtypes.bfloat16), "w": rng.standard_normal((N, 128, F), dtype=np.float32).astype(ml_dtypes.bfloat16)}
def setup_inputs_big(rng):
    d = setup_inputs(rng)
    for k in ("a", "w"): d[k] = (d[k].astype(np.float32) * 1024.0).astype(d[k].dtype)
    return d
def setup_inputs_small(rng):
    d = setup_inputs(rng)
    for k in ("a", "w"): d[k] = (d[k].astype(np.float32) * (1 / 1024.0)).astype(d[k].dtype)
    return d
def setup_inputs_apart(rng):
    d = setup_inputs(rng)
    f = (10.0 ** rng.permutation(np.linspace(-1.5, 1.5, N))).astype(np.float32).reshape(N, 1, 1)
    for k in ("a", "w"): d[k] = (d[k].astype(np.float32) * f).astype(d[k].dtype)
    return d
def reference(a, w):
    A, W = a.astype(np.float64), w.astype(np.float64)
    p = [A[j].T @ W[j] for j in range(N)]
    y = np.stack([sum(p[r - i] for i in range(WB + 1) if r - i >= 0) for r in range(N)])
    return {"y": y.astype(ml_dtypes.bfloat16 if a.dtype != np.float64 else np.float64)}

from concourse.mybir import AluOpType

F = 64
ENGINES = 8

SCRATCH = {
    "a_sb": ("sbuf", [128, 128], "bfloat16"),
    "w_sb": ("sbuf", [128, F], "bfloat16"),
    "p_ps": ("psum", [128, F], "float32"),
    "send": ("sbuf", [128, F], "bfloat16"),
    "land": ("sbuf", [128, F], "bfloat16"),
    "y_sb": ("sbuf", [128, F], "bfloat16"),
}
SEMAPHORES = ["loaded", "mm", "cp", "sent", "arrived", "added", "stored"]


def pick_engines(allowed, n):
    bits = [b for b in range(allowed.bit_length()) if (allowed >> b) & 1]
    n = min(n, len(bits))
    chosen = bits[::len(bits) // n][:n]
    m = 0
    for b in chosen:
        m |= 1 << b
    return m, n


def rank_program(g, core, T, topo):
    rank = T.rank_of(core)
    if rank is None:
        return
    cores = T.cores
    last = len(cores) - 1
    s = T.sem
    sends = rank < last
    receives = rank > 0

    g.sync.dma_start(T.a_sb[:], T.a[:]).then_inc(s.loaded, 16)
    g.scalar.dma_start(T.w_sb[:], T.w[:]).then_inc(s.loaded, 16)

    g.tensor.wait_ge(s.loaded, 32)
    g.tensor.matmul(T.p_ps[:], T.a_sb[:], T.w_sb[:], True, True).then_inc(s.mm, 1)

    g.vector.wait_ge(s.mm, 1)
    if sends:
        dst = cores[rank + 1]
        assert topo.may_write(core, dst)
        mask, n_out = pick_engines(topo.mask(core, dst), ENGINES)
        rid, pid, _ = topo.addr(dst)
        g.vector.tensor_copy(T.send[:], T.p_ps[:]).then_inc(s.cp, 1)
        g.wait_ge(s.cp, 1)
        g.remote_dma(out_ap=T.land[:], in_ap=T.send[:], remote_sem=s.arrived, local_sem=s.sent,
                     pid=pid, routing_id=rid, dma_engine_mask=mask)

    if receives:
        src = cores[rank - 1]
        _, n_in = pick_engines(topo.mask(src, core), ENGINES)
        g.vector.wait_ge(s.arrived, n_in)
        g.vector.tensor_tensor(T.y_sb[:], T.p_ps[:], T.land[:], AluOpType.add).then_inc(s.added, 1)
        g.sync.wait_ge(s.added, 1)
        g.sync.dma_start(T.y[:], T.y_sb[:]).then_inc(s.stored, 16)
        if sends:
            g.wait_ge(s.sent, n_out)
    else:
        g.sync.wait_ge(s.sent, n_out)
        g.sync.dma_start(T.y[:], T.send[:]).then_inc(s.stored, 16)
    g.sync.wait_ge(s.stored, 16)
